import numpy as np
import ml_dtypes


def mxq(x, axis, fmt="e4m3"):
    dtype, down = {"e4m3": (ml_dtypes.float8_e4m3fn, 7), "e5m2": (ml_dtypes.float8_e5m2, 14)}[fmt]
    v = np.moveaxis(np.asarray(x, np.float32).astype(ml_dtypes.bfloat16).astype(np.float64), axis, -1)
    blocks = v.reshape(v.shape[:-1] + (-1, 32))
    amax = np.abs(blocks).max(-1, keepdims=True)
    byte = np.maximum(np.where(amax > 0, np.frexp(amax)[1] - 1 + 127, 0) - down, 1)
    scale = np.exp2(byte - 127.0)
    codes = (blocks / scale).astype(np.float32).astype(dtype).astype(np.float64)
    return np.moveaxis((codes * scale).reshape(v.shape), -1, axis)


WIDE = False


def mx_kscale(k, group=512):
    if not WIDE:
        return np.ones(k)
    levels = np.array([18, -18])
    if group != 512:
        return np.exp2(np.random.permutation(np.resize(levels, k // group))).repeat(group)
    if k % 512:
        return np.exp2(np.random.permutation(np.resize(levels, k // 32))).repeat(32)
    a = np.empty((k // 512, 16))
    for p in range(k // 512):
        a[p, :8] = np.random.permutation(np.resize(levels, 8))
        for g in range(8):
            far = levels[np.abs(levels - a[p, g]) >= 10]
            a[p, g + 8] = far[np.random.randint(len(far))]
    return np.exp2(a.ravel()).repeat(32)


def f64(x):
    return np.asarray(x).astype(np.float64)


G, D, M, N = 8, 128, 128, 512


def setup_inputs():
    n = np.random.standard_normal
    s_d = mx_kscale(D, 0)
    return {
        "x": (n((D, N)) * s_d[:, None]).astype(np.float32),
        "w": (n((G, D, M)) / np.sqrt(D) / s_d[:, None]).astype(np.float32),
        "b": (0.5 * n((G, M, 1))).astype(np.float32),
        "gt": (np.random.dirichlet(np.ones(G), N).T[:, None, :]).astype(np.float32),
    }


def reference(x, w, b, gt):
    wq = mxq(f64(w), 1, "e4m3")
    xq = mxq(f64(x), 0, "e4m3")
    z = wq.transpose(0, 2, 1) @ xq
    y = np.maximum(z + f64(b), 0.0) * f64(gt)
    s = y.sum(0)
    return s

@@ -1,0 +1,182 @@
+from contextlib import ExitStack
+
+import concourse.mybir as mybir
+
+G, D, M, N = 8, 128, 128, 512
+FLOPS = 2 * G * D * M * N
+
+F32 = mybir.dt.float32
+BF16 = mybir.dt.bfloat16
+I32 = mybir.dt.int32
+U32 = mybir.dt.uint32
+U8 = mybir.dt.uint8
+FP8X4 = mybir.dt.float8_e4m3fn_x4
+ALU = mybir.AluOpType
+ACT = mybir.ActivationFunctionType
+
+P = 128
+PACK = 4
+ROWS = 32
+TILES = 4
+HALF = N // 2
+QUART = 128
+
+
+def tile_rows_mexp_soft_kernel(tc, x, w, b, gt, out):
+    nc = tc.nc
+    with ExitStack() as ctx:
+        sb = ctx.enter_context(tc.tile_pool(name="sb", bufs=1))
+        ps = ctx.enter_context(tc.psum_pool(name="ps", bufs=1))
+        ctx.enter_context(tc.manual_schedule())
+
+        w_raw = [sb.tile([P, PACK * M], F32, name="w_raw%d" % s) for s in range(2)]
+        w_bf = [sb.tile([P, PACK * M], BF16, name="w_bf%d" % s, align_bytes=64) for s in range(2)]
+        w_codes = [sb.tile([P, M], U32, name="w_codes%d" % s, align_bytes=64) for s in range(2)]
+        w_scales = [sb.tile([P, M], U8, name="w_scales%d" % s, align_bytes=64) for s in range(2)]
+        x_raw = sb.tile([P, PACK, HALF], F32)
+        x_bf = [sb.tile([P, PACK * QUART], BF16, name="x_bf%d" % q, align_bytes=64) for q in range(2)]
+        x_mx = [sb.tile([P, HALF + HALF // 4], U32, name="x_mx%d" % s, align_bytes=64) for s in range(2)]
+        b_rows = sb.tile([P, G * 32], F32, align_bytes=64)
+        b_cols = sb.tile([P, G * 32], F32, align_bytes=64)
+        banks = [ps.tile([P, N], F32, name="bank%d" % g) for g in range(G)]
+
+        pieces = [(0, 0), (1, 1), (2, 0), (3, 1), (0, 1), (2, 1), (1, 0), (3, 0)]
+        gates = {pc: sb.tile([P, 2, HALF], F32, name="gate%d%d" % pc) for pc in pieces}
+        ys = {pc: sb.tile([P, 2, HALF], F32, name="y%d%d" % pc) for pc in pieces}
+        res = sb.tile([P, N], F32)
+        fold = sb.tile([P, HALF], F32)
+        last = sb.tile([P, HALF], F32)
+
+        def load_w(s):
+            nc.sync.dma_start(out=w_raw[s][:], in_=w[4 * s : 4 * s + 4].rearrange("r (p j) m -> (r p) (j m)", j=PACK))
+
+        def load_x(eng, r):
+            h = r // 2
+            eng.dma_start(
+                out=x_raw[ROWS * r : ROWS * (r + 1), :, :],
+                in_=x[:, h * HALF : (h + 1) * HALF].rearrange("(p j) n -> p j n", j=PACK),
+            )
+
+        def load_gate(pc):
+            pair, h = pc
+            nc.sync.dma_start(
+                out=gates[pc][:],
+                in_=gt[2 * pair : 2 * pair + 2, 0, h * HALF : (h + 1) * HALF].partition_broadcast(P),
+            )
+
+        nc.vector.memset(b_rows[:], 0.0)
+        nc.vector.memset(x_mx[0][:, HALF:], 0)
+
+        load_w(0)
+        load_x(nc.scalar, 2)
+        load_x(nc.sync, 0)
+        load_x(nc.scalar, 3)
+        load_x(nc.sync, 1)
+        nc.scalar.dma_start(
+            out=b_rows[0:P:32, :].rearrange("q (g j) -> q g j", j=32),
+            in_=b.rearrange("g (q j) o -> q g (j o)", j=32),
+        )
+        load_w(1)
+        for pc in pieces[:3]:
+            load_gate(pc)
+
+        def spread(copy, dst, src):
+            copy(
+                out=dst.rearrange("p (c i t) -> p c t i", i=4, t=PACK),
+                in_=src.rearrange("p t (c i) -> p c t i", i=4),
+            )
+
+        def spread_w(s):
+            spread(nc.scalar.copy, w_bf[s][:], w_raw[s][:].rearrange("p (t m) -> p t m", t=PACK))
+
+        def quant_w(s):
+            nc.vector.quantize_mx(out=w_codes[s][:].bitcast(FP8X4), scales=w_scales[s][:], in_=w_bf[s][:])
+
+        def x_codes(stage, q):
+            return x_mx[stage][:, q * QUART : (q + 1) * QUART]
+
+        def x_scales(stage, q):
+            return x_mx[stage][:, HALF + q * QUART // 4 : HALF + (q + 1) * QUART // 4].bitcast(U8)
+
+        def experts(pc):
+            pair, h = pc
+            for e in range(2):
+                g = 2 * pair + e
+                s, r = divmod(g, TILES)
+                stage = 0 if r // 2 == h else 1
+                rows = slice(ROWS * r, ROWS * (r + 1))
+                for q in range(2):
+                    c0 = h * HALF + q * QUART
+                    nc.tensor.matmul_mx(
+                        out=banks[g][:, c0 : c0 + QUART],
+                        lhsT=w_codes[s][rows, :].bitcast(FP8X4),
+                        lhsT_scale=w_scales[s][rows, :],
+                        rhs=x_codes(stage, q)[rows, :].bitcast(FP8X4),
+                        rhs_scale=x_scales(stage, q)[rows, :],
+                        start=True,
+                        stop=True,
+                    )
+
+        def relu(pc):
+            pair, h = pc
+            for e in range(2):
+                g = 2 * pair + e
+                nc.scalar.activation(
+                    out=ys[pc][:, e, :],
+                    in_=banks[g][:, h * HALF : (h + 1) * HALF],
+                    func=ACT.Relu,
+                    bias=b_cols[:, 32 * g : 32 * g + 1],
+                )
+
+        def gate(pc):
+            nc.vector.tensor_tensor(out=ys[pc][:], in0=ys[pc][:], in1=gates[pc][:], op=ALU.mult)
+
+        def add(dst, a, c):
+            nc.vector.tensor_tensor(out=dst, in0=a, in1=c, op=ALU.add)
+
+        spread_w(0)
+        nc.vector.transpose(out=b_cols[:], in_=b_rows[:])
+        quant_w(0)
+        for q in range(2):
+            spread(nc.vector.tensor_copy, x_bf[q][:], x_raw[:, :, q * QUART : (q + 1) * QUART])
+        spread_w(1)
+        for q in range(2):
+            nc.vector.quantize_mx(out=x_codes(0, q).bitcast(FP8X4), scales=x_scales(0, q), in_=x_bf[q][:])
+        quant_w(1)
+        nc.scalar.dma_start(out=x_mx[1][64:128, :].bitcast(I32), in_=x_mx[0][0:64, :].bitcast(I32))
+        nc.scalar.dma_start(out=x_mx[1][0:64, :].bitcast(I32), in_=x_mx[0][64:128, :].bitcast(I32))
+        for pc in pieces[3:]:
+            load_gate(pc)
+
+        for pc in pieces[:4]:
+            experts(pc)
+        for pc in pieces[:4]:
+            relu(pc)
+        for pc in pieces[4:]:
+            experts(pc)
+            relu(pc)
+
+        p00, p11, p20, p31, p01, p21, p10, p30 = pieces
+        gate(p00)
+        gate(p11)
+        gate(p20)
+        gate(p31)
+        add(ys[p00][:], ys[p00][:], ys[p20][:])
+        gate(p01)
+        add(ys[p11][:], ys[p11][:], ys[p31][:])
+        gate(p21)
+        add(ys[p11][:], ys[p11][:], ys[p01][:])
+        gate(p10)
+        add(ys[p11][:], ys[p11][:], ys[p21][:])
+        add(ys[p00][:], ys[p00][:], ys[p10][:])
+        add(res[:, HALF:], ys[p11][:, 0, :], ys[p11][:, 1, :])
+        nc.sync.dma_start(out=out[:, HALF:], in_=res[:, HALF:])
+        gate(p30)
+        add(fold[:], ys[p00][:, 0, :], ys[p00][:, 1, :])
+        for q in range(2):
+            cols = slice(q * QUART, (q + 1) * QUART)
+            add(last[:, cols], ys[p30][:, 0, cols], ys[p30][:, 1, cols])
+        for q in range(2):
+            cols = slice(q * QUART, (q + 1) * QUART)
+            add(res[:, cols], fold[:, cols], last[:, cols])
+        nc.sync.dma_start(out=out[:, :HALF], in_=res[:, :HALF])

@@ -40,28 +40,29 @@ def tile_rows_mexp_soft_kernel(tc, x, w, b, gt, out):
         b_cols = sb.tile([P, G * 32], F32, align_bytes=64)
         banks = [ps.tile([P, N], F32, name="bank%d" % g) for g in range(G)]
 
-        pieces = [(0, 0), (1, 1), (2, 0), (3, 1), (0, 1), (2, 1), (1, 0), (3, 0)]
-        gates = {pc: sb.tile([P, 2, HALF], F32, name="gate%d%d" % pc) for pc in pieces}
-        ys = {pc: sb.tile([P, 2, HALF], F32, name="y%d%d" % pc) for pc in pieces}
+        gate_own = sb.tile([P, 4, N], F32)
+        gate_other = sb.tile([P, 3, N], F32)
+        gate_ends = sb.tile([P, 2, HALF], F32)
+        gt_flat = gt.rearrange("g o n -> (g o n)")
+
+        runs = [[(2 * k, 1), (2 * k + 1, 0)] for k in range(4)]
+        runs = runs + [[(2 * k + 1, 1), (2 * k + 2, 0)] for k in range(3)] + [[(0, 0), (G - 1, 1)]]
+        gates = [gate_own[:, k, :] for k in range(4)] + [gate_other[:, k, :] for k in range(3)]
+        gates = gates + [gate_ends[:].rearrange("p e n -> p (e n)")]
+        ys = [sb.tile([P, N], F32, name="y%d" % k) for k in range(G)]
         res = sb.tile([P, N], F32)
-        fold = sb.tile([P, HALF], F32)
-        last = sb.tile([P, HALF], F32)
 
         def load_w(s):
             nc.sync.dma_start(out=w_raw[s][:], in_=w[4 * s : 4 * s + 4].rearrange("r (p j) m -> (r p) (j m)", j=PACK))
 
+        def own_half(r):
+            return 1 - r % 2
+
         def load_x(eng, r):
-            h = r // 2
+            h = own_half(r)
             eng.dma_start(
                 out=x_raw[ROWS * r : ROWS * (r + 1), :, :],
                 in_=x[:, h * HALF : (h + 1) * HALF].rearrange("(p j) n -> p j n", j=PACK),
-            )
-
-        def load_gate(pc):
-            pair, h = pc
-            nc.sync.dma_start(
-                out=gates[pc][:],
-                in_=gt[2 * pair : 2 * pair + 2, 0, h * HALF : (h + 1) * HALF].partition_broadcast(P),
             )
 
         nc.vector.memset(b_rows[:], 0.0)
@@ -77,8 +78,18 @@ def tile_rows_mexp_soft_kernel(tc, x, w, b, gt, out):
             in_=b.rearrange("g (q j) o -> q g (j o)", j=32),
         )
         load_w(1)
-        for pc in pieces[:3]:
-            load_gate(pc)
+        nc.sync.dma_start(
+            out=gate_own[:],
+            in_=gt_flat.rearrange("(k n) -> k n", k=4)[:, HALF : HALF + N].partition_broadcast(P),
+        )
+        nc.sync.dma_start(
+            out=gate_other[:],
+            in_=gt_flat[N : N + 3 * 2 * N].rearrange("(k n) -> k n", k=3)[:, HALF : HALF + N].partition_broadcast(P),
+        )
+        nc.sync.dma_start(
+            out=gate_ends[:],
+            in_=gt_flat.rearrange("(k n) -> k n", n=HALF)[0 : 2 * G : 2 * G - 1, :].partition_broadcast(P),
+        )
 
         def spread(copy, dst, src):
             copy(
@@ -98,12 +109,10 @@ def tile_rows_mexp_soft_kernel(tc, x, w, b, gt, out):
         def x_scales(stage, q):
             return x_mx[stage][:, HALF + q * QUART // 4 : HALF + (q + 1) * QUART // 4].bitcast(U8)
 
-        def experts(pc):
-            pair, h = pc
-            for e in range(2):
-                g = 2 * pair + e
+        def experts(k):
+            for g, h in runs[k]:
                 s, r = divmod(g, TILES)
-                stage = 0 if r // 2 == h else 1
+                stage = 0 if own_half(r) == h else 1
                 rows = slice(ROWS * r, ROWS * (r + 1))
                 for q in range(2):
                     c0 = h * HALF + q * QUART
@@ -117,66 +126,51 @@ def tile_rows_mexp_soft_kernel(tc, x, w, b, gt, out):
                         stop=True,
                     )
 
-        def relu(pc):
-            pair, h = pc
-            for e in range(2):
-                g = 2 * pair + e
+        def relu(k):
+            for e, (g, h) in enumerate(runs[k]):
                 nc.scalar.activation(
-                    out=ys[pc][:, e, :],
+                    out=ys[k][:, e * HALF : (e + 1) * HALF],
                     in_=banks[g][:, h * HALF : (h + 1) * HALF],
                     func=ACT.Relu,
                     bias=b_cols[:, 32 * g : 32 * g + 1],
                 )
 
-        def gate(pc):
-            nc.vector.tensor_tensor(out=ys[pc][:], in0=ys[pc][:], in1=gates[pc][:], op=ALU.mult)
+        def gate(k, cols=slice(0, N)):
+            nc.vector.tensor_tensor(out=ys[k][:, cols], in0=ys[k][:, cols], in1=gates[k][:, cols], op=ALU.mult)
 
         def add(dst, a, c):
             nc.vector.tensor_tensor(out=dst, in0=a, in1=c, op=ALU.add)
 
         spread_w(0)
-        nc.vector.transpose(out=b_cols[:], in_=b_rows[:])
         quant_w(0)
         for q in range(2):
             spread(nc.vector.tensor_copy, x_bf[q][:], x_raw[:, :, q * QUART : (q + 1) * QUART])
         spread_w(1)
         for q in range(2):
             nc.vector.quantize_mx(out=x_codes(0, q).bitcast(FP8X4), scales=x_scales(0, q), in_=x_bf[q][:])
+        nc.vector.transpose(out=b_cols[:], in_=b_rows[:])
         quant_w(1)
-        nc.scalar.dma_start(out=x_mx[1][64:128, :].bitcast(I32), in_=x_mx[0][0:64, :].bitcast(I32))
-        nc.scalar.dma_start(out=x_mx[1][0:64, :].bitcast(I32), in_=x_mx[0][64:128, :].bitcast(I32))
-        for pc in pieces[3:]:
-            load_gate(pc)
+        nc.scalar.dma_start(out=x_mx[1][0:64, :].bitcast(I32), in_=x_mx[0][32:96, :].bitcast(I32))
+        nc.scalar.dma_start(out=x_mx[1][64:128, :].bitcast(I32), in_=x_mx[0][32:96, :].bitcast(I32))
 
-        for pc in pieces[:4]:
-            experts(pc)
-        for pc in pieces[:4]:
-            relu(pc)
-        for pc in pieces[4:]:
-            experts(pc)
-            relu(pc)
+        for k in range(4):
+            experts(k)
+        for k in range(4):
+            relu(k)
+        for k in range(4, G):
+            experts(k)
+            relu(k)
 
-        p00, p11, p20, p31, p01, p21, p10, p30 = pieces
-        gate(p00)
-        gate(p11)
-        gate(p20)
-        gate(p31)
-        add(ys[p00][:], ys[p00][:], ys[p20][:])
-        gate(p01)
-        add(ys[p11][:], ys[p11][:], ys[p31][:])
-        gate(p21)
-        add(ys[p11][:], ys[p11][:], ys[p01][:])
-        gate(p10)
-        add(ys[p11][:], ys[p11][:], ys[p21][:])
-        add(ys[p00][:], ys[p00][:], ys[p10][:])
-        add(res[:, HALF:], ys[p11][:, 0, :], ys[p11][:, 1, :])
-        nc.sync.dma_start(out=out[:, HALF:], in_=res[:, HALF:])
-        gate(p30)
-        add(fold[:], ys[p00][:, 0, :], ys[p00][:, 1, :])
-        for q in range(2):
-            cols = slice(q * QUART, (q + 1) * QUART)
-            add(last[:, cols], ys[p30][:, 0, cols], ys[p30][:, 1, cols])
-        for q in range(2):
-            cols = slice(q * QUART, (q + 1) * QUART)
-            add(res[:, cols], fold[:, cols], last[:, cols])
-        nc.sync.dma_start(out=out[:, :HALF], in_=res[:, :HALF])
+        low, high = slice(0, HALF), slice(HALF, N)
+        gate(0)
+        gate(1)
+        for k in range(2, G - 1):
+            gate(k)
+            add(ys[0][:], ys[0][:], ys[k - 1][:])
+        gate(G - 1, low)
+        add(ys[0][:], ys[0][:], ys[G - 2][:])
+        gate(G - 1, high)
+        add(res[:, low], ys[0][:, high], ys[G - 1][:, low])
+        nc.sync.dma_start(out=out[:, low], in_=res[:, low])
+        add(res[:, high], ys[0][:, low], ys[G - 1][:, high])
+        nc.scalar.dma_start(out=out[:, high], in_=res[:, high])

@@ -19,7 +19,8 @@ PACK = 4
 ROWS = 32
 TILES = 4
 HALF = N // 2
-QUART = 128
+COLS = 128
+BLK = 32
 
 
 def tile_rows_mexp_soft_kernel(tc, x, w, b, gt, out):
@@ -34,29 +35,27 @@ def tile_rows_mexp_soft_kernel(tc, x, w, b, gt, out):
         w_codes = [sb.tile([P, M], U32, name="w_codes%d" % s, align_bytes=64) for s in range(2)]
         w_scales = [sb.tile([P, M], U8, name="w_scales%d" % s, align_bytes=64) for s in range(2)]
         x_raw = sb.tile([P, PACK, HALF], F32)
-        x_bf = [sb.tile([P, PACK * QUART], BF16, name="x_bf%d" % q, align_bytes=64) for q in range(2)]
+        x_bf = [sb.tile([P, PACK * COLS], BF16, name="x_bf%d" % t, align_bytes=64) for t in range(2)]
         x_mx = [sb.tile([P, HALF + HALF // 4], U32, name="x_mx%d" % s, align_bytes=64) for s in range(2)]
-        b_rows = sb.tile([P, G * 32], F32, align_bytes=64)
-        b_cols = sb.tile([P, G * 32], F32, align_bytes=64)
+        b_rows = sb.tile([P, BLK], F32, align_bytes=64)
+        b_cols = sb.tile([P, BLK], F32, align_bytes=64)
+        b_wide = [sb.tile([P, 4 * M], F32, name="b_wide%d" % s, align_bytes=64) for s in range(2)]
+        bias = [sb.tile([P, 4 * M], F32, name="bias%d" % s, align_bytes=64) for s in range(2)]
+        g_rows = sb.tile([P, BLK], F32, align_bytes=64)
+        gate = sb.tile([P, BLK], F32, align_bytes=64)
         banks = [ps.tile([P, N], F32, name="bank%d" % g) for g in range(G)]
 
-        gate_own = sb.tile([P, 4, N], F32)
-        gate_other = sb.tile([P, 3, N], F32)
-        gate_ends = sb.tile([P, 2, HALF], F32)
-        gt_flat = gt.rearrange("g o n -> (g o n)")
+        def own_half(r):
+            return r // 2
 
-        runs = [[(2 * k, 1), (2 * k + 1, 0)] for k in range(4)]
-        runs = runs + [[(2 * k + 1, 1), (2 * k + 2, 0)] for k in range(3)] + [[(0, 0), (G - 1, 1)]]
-        gates = [gate_own[:, k, :] for k in range(4)] + [gate_other[:, k, :] for k in range(3)]
-        gates = gates + [gate_ends[:].rearrange("p e n -> p (e n)")]
-        ys = [sb.tile([P, N], F32, name="y%d" % k) for k in range(G)]
-        res = sb.tile([P, N], F32)
+        pieces = [(g, own_half(g % TILES)) for g in range(G)]
+        pieces = pieces + [(g, h) for h in (1, 0) for g in range(G) if own_half(g % TILES) != h]
+        pre = [sb.tile([P, HALF], F32, name="pre%d" % k) for k in range(2 * G)]
+        acc = [sb.tile([P, HALF], F32, name="acc%d" % h, align_bytes=64) for h in range(2)]
+        res = [sb.tile([P, HALF], F32, name="res%d" % h, align_bytes=64) for h in range(2)]
 
         def load_w(s):
             nc.sync.dma_start(out=w_raw[s][:], in_=w[4 * s : 4 * s + 4].rearrange("r (p j) m -> (r p) (j m)", j=PACK))
-
-        def own_half(r):
-            return 1 - r % 2
 
         def load_x(eng, r):
             h = own_half(r)
@@ -65,112 +64,130 @@ def tile_rows_mexp_soft_kernel(tc, x, w, b, gt, out):
                 in_=x[:, h * HALF : (h + 1) * HALF].rearrange("(p j) n -> p j n", j=PACK),
             )
 
-        nc.vector.memset(b_rows[:], 0.0)
         nc.vector.memset(x_mx[0][:, HALF:], 0)
-
+        nc.scalar.dma_start(
+            out=b_rows[:], in_=b.rearrange("g (c a) o -> (g c) (a o)", a=BLK).partition_broadcast(4)
+        )
         load_w(0)
         load_x(nc.scalar, 2)
         load_x(nc.sync, 0)
         load_x(nc.scalar, 3)
         load_x(nc.sync, 1)
-        nc.scalar.dma_start(
-            out=b_rows[0:P:32, :].rearrange("q (g j) -> q g j", j=32),
-            in_=b.rearrange("g (q j) o -> q g (j o)", j=32),
-        )
         load_w(1)
-        nc.sync.dma_start(
-            out=gate_own[:],
-            in_=gt_flat.rearrange("(k n) -> k n", k=4)[:, HALF : HALF + N].partition_broadcast(P),
-        )
-        nc.sync.dma_start(
-            out=gate_other[:],
-            in_=gt_flat[N : N + 3 * 2 * N].rearrange("(k n) -> k n", k=3)[:, HALF : HALF + N].partition_broadcast(P),
-        )
-        nc.sync.dma_start(
-            out=gate_ends[:],
-            in_=gt_flat.rearrange("(k n) -> k n", n=HALF)[0 : 2 * G : 2 * G - 1, :].partition_broadcast(P),
-        )
-
-        def spread(copy, dst, src):
-            copy(
-                out=dst.rearrange("p (c i t) -> p c t i", i=4, t=PACK),
-                in_=src.rearrange("p t (c i) -> p c t i", i=4),
-            )
+        gt_parts = gt.rearrange("g o (h q t j) -> q (g o h) t j", h=2, q=4, t=2)
+        for q in range(4):
+            nc.sync.dma_start(out=g_rows[BLK * q : BLK * (q + 1), :], in_=gt_parts[q])
 
         def spread_w(s):
-            spread(nc.scalar.copy, w_bf[s][:], w_raw[s][:].rearrange("p (t m) -> p t m", t=PACK))
+            nc.scalar.copy(
+                out=w_bf[s][:].rearrange("p (c i j) -> p c j i", i=4, j=PACK),
+                in_=w_raw[s][:].rearrange("p (j c i) -> p c j i", i=4, j=PACK),
+            )
+
+        def spread_x(t):
+            nc.vector.tensor_copy(
+                out=x_bf[t][:].rearrange("p (q c i j) -> p q c j i", q=4, i=4, j=PACK),
+                in_=x_raw[:].rearrange("p j (q t c i) -> p t q c j i", q=4, t=2, i=4)[:, t],
+            )
 
         def quant_w(s):
             nc.vector.quantize_mx(out=w_codes[s][:].bitcast(FP8X4), scales=w_scales[s][:], in_=w_bf[s][:])
 
-        def x_codes(stage, q):
-            return x_mx[stage][:, q * QUART : (q + 1) * QUART]
+        def x_codes(stage, t):
+            return x_mx[stage][:, t * COLS : (t + 1) * COLS]
 
-        def x_scales(stage, q):
-            return x_mx[stage][:, HALF + q * QUART // 4 : HALF + (q + 1) * QUART // 4].bitcast(U8)
+        def x_scales(stage, t):
+            return x_mx[stage][:, HALF + t * COLS // 4 : HALF + (t + 1) * COLS // 4].bitcast(U8)
 
-        def experts(k):
-            for g, h in runs[k]:
-                s, r = divmod(g, TILES)
-                stage = 0 if own_half(r) == h else 1
-                rows = slice(ROWS * r, ROWS * (r + 1))
-                for q in range(2):
-                    c0 = h * HALF + q * QUART
-                    nc.tensor.matmul_mx(
-                        out=banks[g][:, c0 : c0 + QUART],
-                        lhsT=w_codes[s][rows, :].bitcast(FP8X4),
-                        lhsT_scale=w_scales[s][rows, :],
-                        rhs=x_codes(stage, q)[rows, :].bitcast(FP8X4),
-                        rhs_scale=x_scales(stage, q)[rows, :],
-                        start=True,
-                        stop=True,
-                    )
+        def widen_bias(copy, s):
+            copy(
+                out=b_wide[s][:].rearrange("p (c j) -> p c j", j=BLK),
+                in_=b_cols[:, 16 * s : 16 * (s + 1)].unsqueeze(2).to_broadcast([P, 16, BLK]),
+            )
 
-        def relu(k):
-            for e, (g, h) in enumerate(runs[k]):
-                nc.scalar.activation(
-                    out=ys[k][:, e * HALF : (e + 1) * HALF],
-                    in_=banks[g][:, h * HALF : (h + 1) * HALF],
-                    func=ACT.Relu,
-                    bias=b_cols[:, 32 * g : 32 * g + 1],
+        def expert(k):
+            g, h = pieces[k]
+            s, r = divmod(g, TILES)
+            stage = 0 if own_half(r) == h else 1
+            rows = slice(ROWS * r, ROWS * (r + 1))
+            for t in range(2):
+                c0 = h * HALF + t * M
+                nc.tensor.matmul_mx(
+                    out=banks[g][:, c0 : c0 + M],
+                    lhsT=x_codes(stage, t)[rows, :].bitcast(FP8X4),
+                    lhsT_scale=x_scales(stage, t)[rows, :],
+                    rhs=w_codes[s][rows, :].bitcast(FP8X4),
+                    rhs_scale=w_scales[s][rows, :],
+                    start=True,
+                    stop=True,
                 )
 
-        def gate(k, cols=slice(0, N)):
-            nc.vector.tensor_tensor(out=ys[k][:, cols], in0=ys[k][:, cols], in1=gates[k][:, cols], op=ALU.mult)
+        def first_of_half(k):
+            return all(pieces[e][1] != pieces[k][1] for e in range(k))
 
-        def add(dst, a, c):
-            nc.vector.tensor_tensor(out=dst, in0=a, in1=c, op=ALU.add)
+        def add_bias(k):
+            g, h = pieces[k]
+            s, r = divmod(g, TILES)
+            nc.vector.tensor_tensor(
+                out=pre[k][:].rearrange("p (t m) -> p t m", t=2),
+                in0=banks[g][:, h * HALF : (h + 1) * HALF].rearrange("p (t m) -> p t m", t=2),
+                in1=bias[s][:, r * M : (r + 1) * M].unsqueeze(1).to_broadcast([P, 2, M]),
+                op=ALU.add,
+            )
+            if not first_of_half(k):
+                nc.scalar.activation(out=pre[k][:], in_=pre[k][:], func=ACT.Relu)
 
-        spread_w(0)
-        quant_w(0)
-        for q in range(2):
-            spread(nc.vector.tensor_copy, x_bf[q][:], x_raw[:, :, q * QUART : (q + 1) * QUART])
-        spread_w(1)
-        for q in range(2):
-            nc.vector.quantize_mx(out=x_codes(0, q).bitcast(FP8X4), scales=x_scales(0, q), in_=x_bf[q][:])
+        def gate_and_add(k):
+            g, h = pieces[k]
+            for t in range(2):
+                col = 4 * g + 2 * h + t
+                sums = acc[h][:].rearrange("p (mb t i) -> p t mb i", t=2, i=BLK)[:, t]
+                vals = pre[k][:, t * M : (t + 1) * M].rearrange("p (mb i) -> p mb i", i=BLK)
+                if first_of_half(k):
+                    nc.vector.tensor_scalar(
+                        out=sums, in0=vals, scalar1=0.0, scalar2=gate[:, col : col + 1], op0=ALU.max, op1=ALU.mult
+                    )
+                else:
+                    nc.vector.scalar_tensor_tensor(
+                        out=sums, in0=vals, scalar=gate[:, col : col + 1], in1=sums, op0=ALU.mult, op1=ALU.add
+                    )
+
+        def store(h):
+            nc.vector.transpose(out=res[h][:], in_=acc[h][:])
+            for q in range(4):
+                c0 = h * HALF + 64 * q
+                (nc.sync, nc.scalar)[q // 2].dma_start(
+                    out=out[:, c0 : c0 + 64].rearrange("(mb i) n -> i mb n", i=BLK),
+                    in_=res[h][BLK * q : BLK * (q + 1), :].rearrange("i (mb n) -> i mb n", mb=4),
+                )
+
         nc.vector.transpose(out=b_cols[:], in_=b_rows[:])
+        widen_bias(nc.vector.tensor_copy, 0)
+        widen_bias(nc.scalar.copy, 1)
+        spread_w(0)
+        nc.vector.transpose(out=bias[0][:], in_=b_wide[0][:])
+        quant_w(0)
+        for t in range(2):
+            spread_x(t)
+        spread_w(1)
+        for t in range(2):
+            nc.vector.quantize_mx(out=x_codes(0, t).bitcast(FP8X4), scales=x_scales(0, t), in_=x_bf[t][:])
+        nc.vector.transpose(out=gate[:], in_=g_rows[:])
         quant_w(1)
-        nc.scalar.dma_start(out=x_mx[1][0:64, :].bitcast(I32), in_=x_mx[0][32:96, :].bitcast(I32))
-        nc.scalar.dma_start(out=x_mx[1][64:128, :].bitcast(I32), in_=x_mx[0][32:96, :].bitcast(I32))
+        nc.vector.transpose(out=bias[1][:], in_=b_wide[1][:])
+        nc.scalar.dma_start(out=x_mx[1][64:128, :].bitcast(I32), in_=x_mx[0][0:64, :].bitcast(I32))
+        nc.scalar.dma_start(out=x_mx[1][0:64, :].bitcast(I32), in_=x_mx[0][64:128, :].bitcast(I32))
 
-        for k in range(4):
-            experts(k)
-        for k in range(4):
-            relu(k)
-        for k in range(4, G):
-            experts(k)
-            relu(k)
-
-        low, high = slice(0, HALF), slice(HALF, N)
-        gate(0)
-        gate(1)
-        for k in range(2, G - 1):
-            gate(k)
-            add(ys[0][:], ys[0][:], ys[k - 1][:])
-        gate(G - 1, low)
-        add(ys[0][:], ys[0][:], ys[G - 2][:])
-        gate(G - 1, high)
-        add(res[:, low], ys[0][:, high], ys[G - 1][:, low])
-        nc.sync.dma_start(out=out[:, low], in_=res[:, low])
-        add(res[:, high], ys[0][:, low], ys[G - 1][:, high])
-        nc.scalar.dma_start(out=out[:, high], in_=res[:, high])
+        lag = 2
+        for k in range(G):
+            expert(k)
+        for k in range(2 * G + lag):
+            if k < 2 * G:
+                if k >= G:
+                    expert(k)
+                add_bias(k)
+            if k == 2 * G:
+                store(1)
+            if k >= lag:
+                gate_and_add(k - lag)
+        store(0)

@@ -21,6 +21,8 @@ TILES = 4
 HALF = N // 2
 COLS = 128
 BLK = 32
+RUN = 4
+OFFLOADED = 5
 
 
 def tile_rows_mexp_soft_kernel(tc, x, w, b, gt, out):
@@ -36,158 +38,165 @@ def tile_rows_mexp_soft_kernel(tc, x, w, b, gt, out):
         w_scales = [sb.tile([P, M], U8, name="w_scales%d" % s, align_bytes=64) for s in range(2)]
         x_raw = sb.tile([P, PACK, HALF], F32)
         x_bf = [sb.tile([P, PACK * COLS], BF16, name="x_bf%d" % t, align_bytes=64) for t in range(2)]
-        x_mx = [sb.tile([P, HALF + HALF // 4], U32, name="x_mx%d" % s, align_bytes=64) for s in range(2)]
-        b_rows = sb.tile([P, BLK], F32, align_bytes=64)
-        b_cols = sb.tile([P, BLK], F32, align_bytes=64)
-        b_wide = [sb.tile([P, 4 * M], F32, name="b_wide%d" % s, align_bytes=64) for s in range(2)]
-        bias = [sb.tile([P, 4 * M], F32, name="bias%d" % s, align_bytes=64) for s in range(2)]
-        g_rows = sb.tile([P, BLK], F32, align_bytes=64)
-        gate = sb.tile([P, BLK], F32, align_bytes=64)
+        x_mx = [sb.tile([P, HALF + HALF // 4], U32, name="x_mx%d" % o, align_bytes=64) for o in range(2)]
+        bias = [sb.tile([P, TILES * M], F32, name="bias%d" % s) for s in range(2)]
+        gate_rows = sb.tile([P, 2 * G * BLK], F32, align_bytes=64)
+        gate_cols = sb.tile([P, 2 * G * BLK], F32, align_bytes=64)
         banks = [ps.tile([P, N], F32, name="bank%d" % g) for g in range(G)]
 
         def own_half(r):
             return r // 2
 
-        pieces = [(g, own_half(g % TILES)) for g in range(G)]
-        pieces = pieces + [(g, h) for h in (1, 0) for g in range(G) if own_half(g % TILES) != h]
-        pre = [sb.tile([P, HALF], F32, name="pre%d" % k) for k in range(2 * G)]
-        acc = [sb.tile([P, HALF], F32, name="acc%d" % h, align_bytes=64) for h in range(2)]
-        res = [sb.tile([P, HALF], F32, name="res%d" % h, align_bytes=64) for h in range(2)]
+        pieces = [(g, own_half(g)) for g in range(TILES)]
+        pieces = pieces + [(TILES + r, own_half(r)) for r in (0, 2, 1, 3)]
+        pieces = pieces + [(TILES * s + r, 1 - own_half(r)) for s in range(2) for r in (2, 0, 3, 1)]
+        opens_half = [all(h != pieces[k][1] for g, h in pieces[:k]) for k in range(len(pieces))]
+
+        gated = {k: sb.tile([P, HALF], F32, name="gated%d" % k) for k in range(OFFLOADED) if not opens_half[k]}
+        hidden = [sb.tile([P, HALF], F32, name="hidden%d" % k) for k in range(len(pieces))]
+        sums = [sb.tile([P, HALF], F32, name="sums%d" % h, align_bytes=64) for h in range(2)]
+        result = [sb.tile([P, HALF], F32, name="result%d" % h, align_bytes=64) for h in range(2)]
 
         def load_w(s):
-            nc.sync.dma_start(out=w_raw[s][:], in_=w[4 * s : 4 * s + 4].rearrange("r (p j) m -> (r p) (j m)", j=PACK))
+            nc.sync.dma_start(
+                out=w_raw[s][:],
+                in_=w[TILES * s : TILES * (s + 1)].rearrange("r (p j) m -> (r p) (j m)", j=PACK),
+            )
 
-        def load_x(eng, r):
+        def load_x(queue, r):
             h = own_half(r)
-            eng.dma_start(
+            queue.dma_start(
                 out=x_raw[ROWS * r : ROWS * (r + 1), :, :],
                 in_=x[:, h * HALF : (h + 1) * HALF].rearrange("(p j) n -> p j n", j=PACK),
             )
 
+        def load_bias(s):
+            nc.sync.dma_start(
+                out=bias[s][:],
+                in_=b[TILES * s : TILES * (s + 1)].rearrange("r m o -> (r m o)").partition_broadcast(P),
+            )
+
+        nc.vector.memset(gate_rows[:], 0.0)
         nc.vector.memset(x_mx[0][:, HALF:], 0)
+        load_x(nc.sync, 0)
+        load_x(nc.scalar, 2)
+        load_x(nc.sync, 1)
+        load_x(nc.scalar, 3)
         nc.scalar.dma_start(
-            out=b_rows[:], in_=b.rearrange("g (c a) o -> (g c) (a o)", a=BLK).partition_broadcast(4)
+            out=gate_rows[0 : P : BLK // 2, :].rearrange("u (c j) -> u c j", j=BLK),
+            in_=gt.rearrange("g o (h u j) -> u (g o h) j", h=2, j=BLK),
         )
         load_w(0)
-        load_x(nc.scalar, 2)
-        load_x(nc.sync, 0)
-        load_x(nc.scalar, 3)
-        load_x(nc.sync, 1)
         load_w(1)
-        gt_parts = gt.rearrange("g o (h q t j) -> q (g o h) t j", h=2, q=4, t=2)
-        for q in range(4):
-            nc.sync.dma_start(out=g_rows[BLK * q : BLK * (q + 1), :], in_=gt_parts[q])
+        load_bias(0)
+        load_bias(1)
 
-        def spread_w(s):
+        def interleave_w(s):
             nc.scalar.copy(
-                out=w_bf[s][:].rearrange("p (c i j) -> p c j i", i=4, j=PACK),
-                in_=w_raw[s][:].rearrange("p (j c i) -> p c j i", i=4, j=PACK),
+                out=w_bf[s][:].rearrange("p (c i j) -> p c j i", i=RUN, j=PACK),
+                in_=w_raw[s][:].rearrange("p (j c i) -> p c j i", i=RUN, j=PACK),
             )
 
-        def spread_x(t):
+        def interleave_x(t):
             nc.vector.tensor_copy(
-                out=x_bf[t][:].rearrange("p (q c i j) -> p q c j i", q=4, i=4, j=PACK),
-                in_=x_raw[:].rearrange("p j (q t c i) -> p t q c j i", q=4, t=2, i=4)[:, t],
+                out=x_bf[t][:].rearrange("p (q c i j) -> p q c j i", q=TILES, i=RUN, j=PACK),
+                in_=x_raw[:].rearrange("p j (q t c i) -> p t q c j i", q=TILES, t=2, i=RUN)[:, t],
             )
 
-        def quant_w(s):
+        def quantise_w(s):
             nc.vector.quantize_mx(out=w_codes[s][:].bitcast(FP8X4), scales=w_scales[s][:], in_=w_bf[s][:])
 
-        def x_codes(stage, t):
-            return x_mx[stage][:, t * COLS : (t + 1) * COLS]
+        def x_codes(other, t):
+            return x_mx[other][:, t * COLS : (t + 1) * COLS]
 
-        def x_scales(stage, t):
-            return x_mx[stage][:, HALF + t * COLS // 4 : HALF + (t + 1) * COLS // 4].bitcast(U8)
+        def x_scales(other, t):
+            return x_mx[other][:, HALF + t * COLS // 4 : HALF + (t + 1) * COLS // 4].bitcast(U8)
 
-        def widen_bias(copy, s):
-            copy(
-                out=b_wide[s][:].rearrange("p (c j) -> p c j", j=BLK),
-                in_=b_cols[:, 16 * s : 16 * (s + 1)].unsqueeze(2).to_broadcast([P, 16, BLK]),
-            )
-
-        def expert(k):
+        def multiply(k):
             g, h = pieces[k]
             s, r = divmod(g, TILES)
-            stage = 0 if own_half(r) == h else 1
+            other = 0 if own_half(r) == h else 1
             rows = slice(ROWS * r, ROWS * (r + 1))
             for t in range(2):
-                c0 = h * HALF + t * M
+                first = h * HALF + t * M
                 nc.tensor.matmul_mx(
-                    out=banks[g][:, c0 : c0 + M],
-                    lhsT=x_codes(stage, t)[rows, :].bitcast(FP8X4),
-                    lhsT_scale=x_scales(stage, t)[rows, :],
+                    out=banks[g][:, first : first + M],
+                    lhsT=x_codes(other, t)[rows, :].bitcast(FP8X4),
+                    lhsT_scale=x_scales(other, t)[rows, :],
                     rhs=w_codes[s][rows, :].bitcast(FP8X4),
                     rhs_scale=w_scales[s][rows, :],
                     start=True,
                     stop=True,
                 )
 
-        def first_of_half(k):
-            return all(pieces[e][1] != pieces[k][1] for e in range(k))
-
-        def add_bias(k):
+        def bias_and_relu(k):
             g, h = pieces[k]
             s, r = divmod(g, TILES)
             nc.vector.tensor_tensor(
-                out=pre[k][:].rearrange("p (t m) -> p t m", t=2),
+                out=hidden[k][:].rearrange("p (t m) -> p t m", t=2),
                 in0=banks[g][:, h * HALF : (h + 1) * HALF].rearrange("p (t m) -> p t m", t=2),
                 in1=bias[s][:, r * M : (r + 1) * M].unsqueeze(1).to_broadcast([P, 2, M]),
                 op=ALU.add,
             )
-            if not first_of_half(k):
-                nc.scalar.activation(out=pre[k][:], in_=pre[k][:], func=ACT.Relu)
+            nc.scalar.activation(out=hidden[k][:], in_=hidden[k][:], func=ACT.Relu)
 
-        def gate_and_add(k):
+        def groups(k, target):
             g, h = pieces[k]
+            found = []
             for t in range(2):
-                col = 4 * g + 2 * h + t
-                sums = acc[h][:].rearrange("p (mb t i) -> p t mb i", t=2, i=BLK)[:, t]
-                vals = pre[k][:, t * M : (t + 1) * M].rearrange("p (mb i) -> p mb i", i=BLK)
-                if first_of_half(k):
-                    nc.vector.tensor_scalar(
-                        out=sums, in0=vals, scalar1=0.0, scalar2=gate[:, col : col + 1], op0=ALU.max, op1=ALU.mult
+                col = BLK * (2 * g + h) + (BLK // 2) * t
+                found.append(
+                    (
+                        target[:].rearrange("p (mb t i) -> p t mb i", t=2, i=BLK)[:, t],
+                        hidden[k][:, t * M : (t + 1) * M].rearrange("p (mb i) -> p mb i", i=BLK),
+                        gate_cols[:, col : col + 1],
                     )
-                else:
-                    nc.vector.scalar_tensor_tensor(
-                        out=sums, in0=vals, scalar=gate[:, col : col + 1], in1=sums, op0=ALU.mult, op1=ALU.add
-                    )
+                )
+            return found
 
-        def store(h):
-            nc.vector.transpose(out=res[h][:], in_=acc[h][:])
-            for q in range(4):
-                c0 = h * HALF + 64 * q
-                (nc.sync, nc.scalar)[q // 2].dma_start(
-                    out=out[:, c0 : c0 + 64].rearrange("(mb i) n -> i mb n", i=BLK),
-                    in_=res[h][BLK * q : BLK * (q + 1), :].rearrange("i (mb n) -> i mb n", mb=4),
+        def gate_on_scalar(k):
+            h = pieces[k][1]
+            for place, values, gate in groups(k, sums[h] if opens_half[k] else gated[k]):
+                nc.scalar.activation(out=place, in_=values, func=ACT.Copy, scale=gate)
+            if not opens_half[k]:
+                nc.gpsimd.tensor_tensor(out=sums[h][:], in0=sums[h][:], in1=gated[k][:], op=ALU.add)
+
+        def gate_on_vector(k):
+            for place, values, gate in groups(k, sums[pieces[k][1]]):
+                nc.vector.scalar_tensor_tensor(
+                    out=place, in0=values, scalar=gate, in1=place, op0=ALU.mult, op1=ALU.add
                 )
 
-        nc.vector.transpose(out=b_cols[:], in_=b_rows[:])
-        widen_bias(nc.vector.tensor_copy, 0)
-        widen_bias(nc.scalar.copy, 1)
-        spread_w(0)
-        nc.vector.transpose(out=bias[0][:], in_=b_wide[0][:])
-        quant_w(0)
+        def store(h):
+            nc.vector.transpose(out=result[h][:], in_=sums[h][:])
+            for q in range(TILES):
+                first = h * HALF + 2 * BLK * q
+                (nc.sync, nc.scalar)[q // 2].dma_start(
+                    out=out[:, first : first + 2 * BLK].rearrange("(mb i) n -> i mb n", i=BLK),
+                    in_=result[h][BLK * q : BLK * (q + 1), :].rearrange("i (mb n) -> i mb n", mb=M // BLK),
+                )
+
         for t in range(2):
-            spread_x(t)
-        spread_w(1)
+            interleave_x(t)
+        interleave_w(0)
+        interleave_w(1)
         for t in range(2):
             nc.vector.quantize_mx(out=x_codes(0, t).bitcast(FP8X4), scales=x_scales(0, t), in_=x_bf[t][:])
-        nc.vector.transpose(out=gate[:], in_=g_rows[:])
-        quant_w(1)
-        nc.vector.transpose(out=bias[1][:], in_=b_wide[1][:])
-        nc.scalar.dma_start(out=x_mx[1][64:128, :].bitcast(I32), in_=x_mx[0][0:64, :].bitcast(I32))
-        nc.scalar.dma_start(out=x_mx[1][0:64, :].bitcast(I32), in_=x_mx[0][64:128, :].bitcast(I32))
+        quantise_w(0)
+        nc.vector.transpose(out=gate_cols[:], in_=gate_rows[:])
+        nc.sync.dma_start(out=x_mx[1][0 : P // 2, :].bitcast(I32), in_=x_mx[0][P // 2 : P, :].bitcast(I32))
+        nc.sync.dma_start(out=x_mx[1][P // 2 : P, :].bitcast(I32), in_=x_mx[0][0 : P // 2, :].bitcast(I32))
 
-        lag = 2
-        for k in range(G):
-            expert(k)
-        for k in range(2 * G + lag):
-            if k < 2 * G:
-                if k >= G:
-                    expert(k)
-                add_bias(k)
-            if k == 2 * G:
-                store(1)
-            if k >= lag:
-                gate_and_add(k - lag)
+        for k in range(len(pieces)):
+            if k == TILES - 2:
+                quantise_w(1)
+            multiply(k)
+            bias_and_relu(k)
+            if 1 <= k < OFFLOADED:
+                gate_on_scalar(k - 1)
+            if k == OFFLOADED - 1:
+                gate_on_scalar(k)
+        for k in range(OFFLOADED, len(pieces)):
+            gate_on_vector(k)
         store(0)
+        store(1)

from contextlib import ExitStack

import concourse.mybir as mybir

G, D, M, N = 8, 128, 128, 512
FLOPS = 2 * G * D * M * N

F32 = mybir.dt.float32
BF16 = mybir.dt.bfloat16
I32 = mybir.dt.int32
U32 = mybir.dt.uint32
U8 = mybir.dt.uint8
FP8X4 = mybir.dt.float8_e4m3fn_x4
ALU = mybir.AluOpType
ACT = mybir.ActivationFunctionType

P = 128
PACK = 4
ROWS = 32
TILES = 4
HALF = N // 2
COLS = 128
BLK = 32
RUN = 4
OFFLOADED = 5


def tile_rows_mexp_soft_kernel(tc, x, w, b, gt, out):
    nc = tc.nc
    with ExitStack() as ctx:
        sb = ctx.enter_context(tc.tile_pool(name="sb", bufs=1))
        ps = ctx.enter_context(tc.psum_pool(name="ps", bufs=1))
        ctx.enter_context(tc.manual_schedule())

        w_raw = [sb.tile([P, PACK * M], F32, name="w_raw%d" % s) for s in range(2)]
        w_bf = [sb.tile([P, PACK * M], BF16, name="w_bf%d" % s, align_bytes=64) for s in range(2)]
        w_codes = [sb.tile([P, M], U32, name="w_codes%d" % s, align_bytes=64) for s in range(2)]
        w_scales = [sb.tile([P, M], U8, name="w_scales%d" % s, align_bytes=64) for s in range(2)]
        x_raw = sb.tile([P, PACK, HALF], F32)
        x_bf = [sb.tile([P, PACK * COLS], BF16, name="x_bf%d" % t, align_bytes=64) for t in range(2)]
        x_mx = [sb.tile([P, HALF + HALF // 4], U32, name="x_mx%d" % o, align_bytes=64) for o in range(2)]
        bias = [sb.tile([P, TILES * M], F32, name="bias%d" % s) for s in range(2)]
        gate_rows = sb.tile([P, 2 * G * BLK], F32, align_bytes=64)
        gate_cols = sb.tile([P, 2 * G * BLK], F32, align_bytes=64)
        banks = [ps.tile([P, N], F32, name="bank%d" % g) for g in range(G)]

        def own_half(r):
            return r // 2

        pieces = [(g, own_half(g)) for g in range(TILES)]
        pieces = pieces + [(TILES + r, own_half(r)) for r in (0, 2, 1, 3)]
        pieces = pieces + [(TILES * s + r, 1 - own_half(r)) for s in range(2) for r in (2, 0, 3, 1)]
        opens_half = [all(h != pieces[k][1] for g, h in pieces[:k]) for k in range(len(pieces))]

        gated = {k: sb.tile([P, HALF], F32, name="gated%d" % k) for k in range(OFFLOADED) if not opens_half[k]}
        hidden = [sb.tile([P, HALF], F32, name="hidden%d" % k) for k in range(len(pieces))]
        sums = [sb.tile([P, HALF], F32, name="sums%d" % h, align_bytes=64) for h in range(2)]
        result = [sb.tile([P, HALF], F32, name="result%d" % h, align_bytes=64) for h in range(2)]

        def load_w(s):
            nc.sync.dma_start(
                out=w_raw[s][:],
                in_=w[TILES * s : TILES * (s + 1)].rearrange("r (p j) m -> (r p) (j m)", j=PACK),
            )

        def load_x(queue, r):
            h = own_half(r)
            queue.dma_start(
                out=x_raw[ROWS * r : ROWS * (r + 1), :, :],
                in_=x[:, h * HALF : (h + 1) * HALF].rearrange("(p j) n -> p j n", j=PACK),
            )

        def load_bias(s):
            nc.sync.dma_start(
                out=bias[s][:],
                in_=b[TILES * s : TILES * (s + 1)].rearrange("r m o -> (r m o)").partition_broadcast(P),
            )

        nc.vector.memset(gate_rows[:], 0.0)
        nc.vector.memset(x_mx[0][:, HALF:], 0)
        load_x(nc.sync, 0)
        load_x(nc.scalar, 2)
        load_x(nc.sync, 1)
        load_x(nc.scalar, 3)
        nc.scalar.dma_start(
            out=gate_rows[0 : P : BLK // 2, :].rearrange("u (c j) -> u c j", j=BLK),
            in_=gt.rearrange("g o (h u j) -> u (g o h) j", h=2, j=BLK),
        )
        load_w(0)
        load_w(1)
        load_bias(0)
        load_bias(1)

        def interleave_w(s):
            nc.scalar.copy(
                out=w_bf[s][:].rearrange("p (c i j) -> p c j i", i=RUN, j=PACK),
                in_=w_raw[s][:].rearrange("p (j c i) -> p c j i", i=RUN, j=PACK),
            )

        def interleave_x(t):
            nc.vector.tensor_copy(
                out=x_bf[t][:].rearrange("p (q c i j) -> p q c j i", q=TILES, i=RUN, j=PACK),
                in_=x_raw[:].rearrange("p j (q t c i) -> p t q c j i", q=TILES, t=2, i=RUN)[:, t],
            )

        def quantise_w(s):
            nc.vector.quantize_mx(out=w_codes[s][:].bitcast(FP8X4), scales=w_scales[s][:], in_=w_bf[s][:])

        def x_codes(other, t):
            return x_mx[other][:, t * COLS : (t + 1) * COLS]

        def x_scales(other, t):
            return x_mx[other][:, HALF + t * COLS // 4 : HALF + (t + 1) * COLS // 4].bitcast(U8)

        def multiply(k):
            g, h = pieces[k]
            s, r = divmod(g, TILES)
            other = 0 if own_half(r) == h else 1
            rows = slice(ROWS * r, ROWS * (r + 1))
            for t in range(2):
                first = h * HALF + t * M
                nc.tensor.matmul_mx(
                    out=banks[g][:, first : first + M],
                    lhsT=x_codes(other, t)[rows, :].bitcast(FP8X4),
                    lhsT_scale=x_scales(other, t)[rows, :],
                    rhs=w_codes[s][rows, :].bitcast(FP8X4),
                    rhs_scale=w_scales[s][rows, :],
                    start=True,
                    stop=True,
                )

        def bias_and_relu(k):
            g, h = pieces[k]
            s, r = divmod(g, TILES)
            nc.vector.tensor_tensor(
                out=hidden[k][:].rearrange("p (t m) -> p t m", t=2),
                in0=banks[g][:, h * HALF : (h + 1) * HALF].rearrange("p (t m) -> p t m", t=2),
                in1=bias[s][:, r * M : (r + 1) * M].unsqueeze(1).to_broadcast([P, 2, M]),
                op=ALU.add,
            )
            nc.scalar.activation(out=hidden[k][:], in_=hidden[k][:], func=ACT.Relu)

        def groups(k, target):
            g, h = pieces[k]
            found = []
            for t in range(2):
                col = BLK * (2 * g + h) + (BLK // 2) * t
                found.append(
                    (
                        target[:].rearrange("p (mb t i) -> p t mb i", t=2, i=BLK)[:, t],
                        hidden[k][:, t * M : (t + 1) * M].rearrange("p (mb i) -> p mb i", i=BLK),
                        gate_cols[:, col : col + 1],
                    )
                )
            return found

        def gate_on_scalar(k):
            h = pieces[k][1]
            for place, values, gate in groups(k, sums[h] if opens_half[k] else gated[k]):
                nc.scalar.activation(out=place, in_=values, func=ACT.Copy, scale=gate)
            if not opens_half[k]:
                nc.gpsimd.tensor_tensor(out=sums[h][:], in0=sums[h][:], in1=gated[k][:], op=ALU.add)

        def gate_on_vector(k):
            for place, values, gate in groups(k, sums[pieces[k][1]]):
                nc.vector.scalar_tensor_tensor(
                    out=place, in0=values, scalar=gate, in1=place, op0=ALU.mult, op1=ALU.add
                )

        def store(h):
            nc.vector.transpose(out=result[h][:], in_=sums[h][:])
            for q in range(TILES):
                first = h * HALF + 2 * BLK * q
                (nc.sync, nc.scalar)[q // 2].dma_start(
                    out=out[:, first : first + 2 * BLK].rearrange("(mb i) n -> i mb n", i=BLK),
                    in_=result[h][BLK * q : BLK * (q + 1), :].rearrange("i (mb n) -> i mb n", mb=M // BLK),
                )

        for t in range(2):
            interleave_x(t)
        interleave_w(0)
        interleave_w(1)
        for t in range(2):
            nc.vector.quantize_mx(out=x_codes(0, t).bitcast(FP8X4), scales=x_scales(0, t), in_=x_bf[t][:])
        quantise_w(0)
        nc.vector.transpose(out=gate_cols[:], in_=gate_rows[:])
        nc.sync.dma_start(out=x_mx[1][0 : P // 2, :].bitcast(I32), in_=x_mx[0][P // 2 : P, :].bitcast(I32))
        nc.sync.dma_start(out=x_mx[1][P // 2 : P, :].bitcast(I32), in_=x_mx[0][0 : P // 2, :].bitcast(I32))

        for k in range(len(pieces)):
            if k == TILES - 2:
                quantise_w(1)
            multiply(k)
            bias_and_relu(k)
            if 1 <= k < OFFLOADED:
                gate_on_scalar(k - 1)
            if k == OFFLOADED - 1:
                gate_on_scalar(k)
        for k in range(OFFLOADED, len(pieces)):
            gate_on_vector(k)
        store(0)
        store(1)
